import numpy as np, ml_dtypes
CORES = [16,17,18,19,20,21,22,23,24,25,26,27,28,29,30,31]
N = 16
ROOT = 0
def setup_inputs(rng):
    return {"x": rng.standard_normal((N, 128, 8), dtype=np.float32).astype(ml_dtypes.bfloat16)}
def reference(x):
    y = np.full(x.shape, np.nan, x.dtype)
    y[ROOT] = x.max(axis=0)
    return {"y": y}

import concourse.bass as bass

ROOT = 16
LAST = 17
TREE = {
    18: [16, 19],
    22: [20, 21, 23],
    26: [24, 25, 27],
    30: [28, 29, 31],
    LAST: [18, 22, 26, 30],
}
NSLOT = 1 + max(len(v) for v in TREE.values())
ON_CHIP_MASK = 0xFFFF
OFF_CHIP_MASK = 0x00FF

SCRATCH = {
    "slots": ("dram", [NSLOT, 128, 8], "bfloat16"),
    "land": ("dram", [128, 8], "bfloat16"),
}
SEMAPHORES = ["loaded", "sent", "arrived", "final", "stored"]


def engines(mask):
    return bin(mask).count("1")


def rank_program(g, core, T, topo):
    if T.rank_of(core) is None:
        return

    def mask_to(src, dst):
        return ON_CHIP_MASK if topo.chip(src) == topo.chip(dst) else OFF_CHIP_MASK

    if core == LAST:
        dst, out_ap, out_sem = ROOT, T.land[:], T.sem.final
    else:
        dst = [p for p, ch in TREE.items() if core in ch][0]
        out_ap, out_sem = T.slots[1 + TREE[dst].index(core)], T.sem.arrived
    rid, pid, _se = topo.addr(dst)
    mask = mask_to(core, dst)

    g.dma_start(T.slots[0], T.x[:]).then_inc(T.sem.loaded, 16)
    g.wait_ge(T.sem.loaded, 16)

    children = TREE.get(core, [])
    if children:
        g.wait_ge(T.sem.arrived, sum(engines(mask_to(c, core)) for c in children))
        g.remote_dma_fused(
            [
                bass.RemoteDMATransfer(
                    dst_ids=[bass.DstId(rid=rid, pnc=pid)],
                    dma_engine_mask=mask,
                    remote_sem=out_sem,
                    srcs=[T.slots[j] for j in range(1 + len(children))],
                    dsts=[out_ap],
                    alu_op=2,
                )
            ],
            local_sem=T.sem.sent,
        )
    else:
        g.remote_dma(out_ap, T.slots[0], out_sem, T.sem.sent, pid, rid, mask)

    if core == ROOT:
        g.wait_ge(T.sem.final, engines(mask_to(LAST, ROOT)))
        g.dma_start(T.y[:], T.land[:]).then_inc(T.sem.stored, 16)
        g.wait_ge(T.sem.stored, 16)
    g.wait_ge(T.sem.sent, engines(mask))
